import numpy as np
import ml_dtypes


def mxq(x, axis, fmt="e4m3"):
    dtype, down = {"e4m3": (ml_dtypes.float8_e4m3fn, 7), "e5m2": (ml_dtypes.float8_e5m2, 14)}[fmt]
    v = np.moveaxis(np.asarray(x, np.float32).astype(ml_dtypes.bfloat16).astype(np.float64), axis, -1)
    blocks = v.reshape(v.shape[:-1] + (-1, 32))
    amax = np.abs(blocks).max(-1, keepdims=True)
    byte = np.maximum(np.where(amax > 0, np.frexp(amax)[1] - 1 + 127, 0) - down, 1)
    scale = np.exp2(byte - 127.0)
    codes = (blocks / scale).astype(np.float32).astype(dtype).astype(np.float64)
    return np.moveaxis((codes * scale).reshape(v.shape), -1, axis)


WIDE = False


def mx_kscale(k):
    if not WIDE:
        return np.ones(k)
    levels = np.array([10, -10, 5, -5, 0])
    if k % 512:
        return np.exp2(np.random.permutation(np.resize(levels, k // 32))).repeat(32)
    a = np.empty((k // 512, 16))
    for p in range(k // 512):
        a[p, :8] = np.random.permutation(np.resize(levels, 8))
        for g in range(8):
            far = levels[np.abs(levels - a[p, g]) >= 10]
            a[p, g + 8] = far[np.random.randint(len(far))]
    return np.exp2(a.ravel()).repeat(32)


def f64(x):
    return np.asarray(x).astype(np.float64)


def striped(idx):
    return np.tile(np.asarray(idx).reshape(-1, 16).T, (8, 1)).astype(np.uint16)


def unstriped(offs):
    return offs[:16].T.reshape(-1).astype(np.int64)


def striped8(idx):
    return np.asarray(idx).reshape(8, -1, 16).transpose(0, 2, 1).reshape(128, -1).astype(np.uint16)


def unstriped8(offs):
    return offs.reshape(8, 16, -1).transpose(0, 2, 1).reshape(8, -1).astype(np.int64)


def pick8(x, idx, run):
    r = np.arange(len(x))
    return x[r[:, None], idx[r % (8 * run) // run]]


E2M1 = np.array([0.0, 0.5, 1.0, 1.5, 2.0, 3.0, 4.0, 6.0, -0.0, -0.5, -1.0, -1.5, -2.0, -3.0, -4.0, -6.0])


def pack_weight(w, fmt):
    k, n = w.shape
    w = f64(np.asarray(w, np.float32).astype(ml_dtypes.bfloat16)).reshape(k // 32, 32, n)
    amax = np.abs(w).max(1)
    if fmt == "e4m3":
        byte = np.frexp(amax)[1] - 1 + 127 - 7
    else:
        mant, ex = np.frexp(amax / 6.0)
        byte = np.where(mant > 0.5, ex, ex - 1) + 127
    byte = np.clip(np.where(amax > 0, byte, 1), 1, 254)
    scaled = (w * np.exp2(127.0 - byte)[:, None, :]).reshape(k, n).astype(np.float32)
    by_word = np.ascontiguousarray(scaled.reshape(k // 512, 128, 4, n).transpose(0, 1, 3, 2))
    if fmt == "e4m3":
        words = by_word.astype(ml_dtypes.float8_e4m3fn).view(np.uint8)
    else:
        c = by_word.astype(ml_dtypes.float4_e2m1fn).view(np.uint8) & 0xF
        words = (c[..., 0::2] | (c[..., 1::2] << 4)).reshape(k // 512, 128, 2 * n)
    return np.ascontiguousarray(words), np.ascontiguousarray(byte.astype(np.uint8).reshape(k // 512, 16, n))


def unpack_weight(words, scales, fmt):
    g, _, n = scales.shape
    words = np.ascontiguousarray(words).reshape(g, 128, n, -1)
    if fmt == "e4m3":
        vals = words.view(ml_dtypes.float8_e4m3fn).astype(np.float64)
    else:
        nib = np.empty((g, 128, n, 4), np.uint8)
        nib[..., 0::2] = words & 0xF
        nib[..., 1::2] = words >> 4
        vals = E2M1[nib]
    vals = vals * np.repeat(np.exp2(scales.astype(np.float64) - 127.0), 8, axis=1)[..., None]
    return vals.transpose(0, 1, 3, 2).reshape(g * 512, n)


K, J, R, T, Z, M, C, O, N, S = 512, 512, 512, 2048, 512, 1024, 1024, 512, 256, 1024


def setup_inputs():
    n = np.random.standard_normal
    idx = np.random.permutation(T)[:J]
    idx2 = np.random.permutation(M)[:J]
    idx3 = np.stack([np.random.permutation(C)[:J] for _ in range(8)])
    idx4 = np.stack([np.random.permutation(C)[:J] for _ in range(8)])
    idx5 = np.stack([np.random.permutation(C)[:O] for _ in range(8)])
    idx6 = np.random.permutation(S)[:N]
    fk = mx_kscale(K)
    fr = mx_kscale(R)
    fz = mx_kscale(Z)
    xtp = pack_weight(n((K, T)) * fk[:, None], "e2m1")
    wp = pack_weight(n((K, R)) * 1 / np.sqrt(K) / fk[:, None] * fr, "e4m3")
    xop = pack_weight(n((Z, M)) / fz[:, None], "e4m3")
    w2p = pack_weight(n((Z, R)) * 1 / np.sqrt(Z) * fz[:, None] * fr, "e2m1")
    vsp = pack_weight(n((R, S)) * 1 / np.sqrt(R) / fr[:, None], "e2m1")
    return {
        "xt_words": xtp[0],
        "xt_scales": xtp[1],
        "w_words": wp[0],
        "w_scales": wp[1],
        "xo_words": xop[0],
        "xo_scales": xop[1],
        "w2_words": w2p[0],
        "w2_scales": w2p[1],
        "sa": (np.random.uniform(0.5, 1.6, (R, 1))).astype(np.float32),
        "vs_words": vsp[0],
        "vs_scales": vsp[1],
        "offs": striped(idx),
        "offs2": striped(idx2),
        "offs3": striped8(idx3),
        "offs4": striped8(idx4),
        "offs5": striped8(idx5),
        "offs6": striped(idx6),
    }


def reference(xt_words, xt_scales, w_words, w_scales, xo_words, xo_scales, w2_words, w2_scales, sa, vs_words, vs_scales, offs, offs2, offs3, offs4, offs5, offs6):
    idx = unstriped(offs)
    idx2 = unstriped(offs2)
    idx3 = unstriped8(offs3)
    idx4 = unstriped8(offs4)
    idx5 = unstriped8(offs5)
    idx6 = unstriped(offs6)
    xtu = unpack_weight(xt_words, xt_scales, "e2m1")
    wu = unpack_weight(w_words, w_scales, "e4m3")
    xou = unpack_weight(xo_words, xo_scales, "e4m3")
    w2u = unpack_weight(w2_words, w2_scales, "e2m1")
    vsu = unpack_weight(vs_words, vs_scales, "e2m1")
    xtidxg = xtu[:, idx]
    a = wu.T @ xtidxg
    xoidx2g = xou[:, idx2]
    b = w2u.T @ xoidx2g
    pw = np.zeros((R, C))
    pw[np.arange(R)[:, None], idx3[np.arange(R) % 512 // 64]] = a
    pv = np.zeros((R, C))
    pv[np.arange(R)[:, None], idx4[np.arange(R) % 512 // 64]] = b
    g1 = np.pad(pv, ((0, 0), (1, 0)))[:, :C]
    pg = pw - g1
    hid = pick8(pg, idx5, 64) * f64(sa)
    vsidx6g = vsu[:, idx6]
    hidq = mxq(hid, 0, "e4m3")
    y = vsidx6g.T @ hidq
    return y

@@ -1,0 +1,170 @@
+from contextlib import ExitStack
+
+import concourse.mybir as mybir
+
+K, J, R, T, Z, M, C, O, N, S = 512, 512, 512, 2048, 512, 1024, 1024, 512, 256, 1024
+FLOPS = 2 * K * R * J + 2 * Z * R * J + 2 * R * N * O
+
+F32 = mybir.dt.float32
+BF16 = mybir.dt.bfloat16
+I32 = mybir.dt.int32
+U32 = mybir.dt.uint32
+U16 = mybir.dt.uint16
+U8 = mybir.dt.uint8
+FP8X4 = mybir.dt.float8_e4m3fn_x4
+FP4X4 = mybir.dt.float4_e2m1fn_x4
+COPY = mybir.ActivationFunctionType.Copy
+SUB = mybir.AluOpType.subtract
+
+P = 128
+PACK = 4
+QUADS = 4
+NOTE_PIECES = (128, 128, 256)
+HALF = O // 2
+
+
+def tile_picked_tokens_plain_two_lagged_store_plain_kernel(
+    tc, xt_words, xt_scales, w_words, w_scales, xo_words, xo_scales, w2_words, w2_scales,
+    sa, vs_words, vs_scales, offs, offs2, offs3, offs4, offs5, offs6, out,
+):
+    nc = tc.nc
+    with ExitStack() as ctx:
+        lists = ctx.enter_context(tc.tile_pool(name="lists", bufs=1))
+        sb = ctx.enter_context(tc.tile_pool(name="sb", bufs=1))
+        psum = ctx.enter_context(tc.psum_pool(name="psum", bufs=1))
+
+        def load_list(name, src):
+            tl = lists.tile(list(src.shape), U16, name=name)
+            nc.sync.dma_start(tl[:], src)
+            return tl
+
+        def load_scale_rows(name, src):
+            width = src.shape[2]
+            plane = sb.tile([P, width], U8, name=name, align_bytes=64)
+            for q in range(QUADS):
+                rows = src[0, 4 * q : 4 * q + 4, :].bitcast(I32)
+                nc.sync.dma_start(plane[32 * q : 32 * q + 32, :].bitcast(I32), rows.partition_broadcast(8))
+            return plane
+
+        def load_words(queue, name, src, width, dtype, tag):
+            tl = sb.tile([P, width], dtype, name=name, tag=tag, align_bytes=64)
+            queue.dma_start(tl[:].bitcast(I32), src.bitcast(I32))
+            return tl
+
+        def deal(engine_copy, name, src, dtype, tag):
+            dealt = sb.tile([P, PACK, P], dtype, name=name, tag=tag, align_bytes=64)
+            engine_copy(dealt[:].rearrange("p t m -> p m t"), src[:].rearrange("p (m t) -> p m t", t=PACK))
+            return dealt
+
+        def entries(tl, first, count):
+            return tl[:, first // 16 : (first + count) // 16]
+
+        w2s_stage = sb.tile([P, QUADS, R // 4], I32, name="w2s_stage")
+        nc.sync.dma_start(w2s_stage[0:4, :, :], w2_scales[0].rearrange("(q j) n -> j q n", j=4).bitcast(I32))
+        l2 = load_list("l2", offs2)
+        xo_sc = load_scale_rows("xo_sc", xo_scales)
+        w2_w = load_words(nc.scalar, "w2_w", w2_words[0], R, U16, "w2_w")
+        xo_w = load_words(nc.scalar, "xo_w", xo_words[0].rearrange("p n t -> p (n t)"), M, U32, "wide0")
+        l4 = load_list("l4", offs4)
+
+        w2_sc = sb.tile([P, R], U8, name="w2_sc", align_bytes=64)
+        nc.vector.memset(w2_sc[:].bitcast(I32), 0)
+        pv = [sb.tile([P, C], F32, name="pv%d" % t) for t in range(PACK - 1)]
+        for board in pv:
+            nc.vector.memset(board[:], 0.0)
+        for q in range(QUADS):
+            nc.vector.tensor_copy(w2_sc[32 * q : 32 * q + 4, :].bitcast(I32), w2s_stage[0:4, q, :])
+        w2_sc_d = deal(nc.vector.tensor_copy, "w2_sc_d", w2_sc, U8, "dealt_scales")
+        w2_w_d = deal(nc.scalar.copy, "w2_w_d", w2_w, U16, "dealt_words")
+
+        b_sb = [sb.tile([P, J], F32, name="b_sb%d" % t) for t in range(PACK)]
+        b_ps = [psum.tile([P, J], F32, name="b_ps%d" % t, tag="bank%d" % t) for t in range(PACK)]
+        first = 0
+        for piece, count in enumerate(NOTE_PIECES):
+            cols = slice(first, first + count)
+            xo_gs = sb.tile([P, count], U8, name="xo_gs%d" % piece, tag="picked_scales%d" % piece, align_bytes=64)
+            xo_gw = sb.tile([P, count], U32, name="xo_gw%d" % piece, tag="picked_words%d" % piece, align_bytes=64)
+            nc.vector.tensor_copy(xo_gs[:], xo_sc[:].indirect(entries(l2, first, count)))
+            nc.vector.tensor_copy(xo_gw[:], xo_w[:].indirect(entries(l2, first, count)))
+            for t in range(PACK):
+                nc.tensor.matmul_mx(
+                    out=b_ps[t][:, cols], lhsT=w2_w_d[:, t, :].bitcast(FP4X4), lhsT_scale=w2_sc_d[:, t, :],
+                    rhs=xo_gw[:].bitcast(FP8X4), rhs_scale=xo_gs[:], start=True, stop=True,
+                )
+                nc.vector.tensor_copy(b_sb[t][:, cols], b_ps[t][:, cols])
+                if len(pv) == t:
+                    pv.append(sb.tile([P, C], F32, name="pv%d" % t, tag="picked_words0", align_bytes=64))
+                    nc.vector.memset(pv[t][:], 0.0)
+                nc.scalar.activation(pv[t][:].indirect(entries(l4, first, count)), b_sb[t][:, cols], COPY)
+            first = first + count
+
+        l1 = load_list("l1", offs)
+        xt_w = load_words(nc.sync, "xt_w", xt_words[0], T, U16, "wide1")
+        w_w = load_words(nc.sync, "w_w", w_words[0].rearrange("p n t -> p (n t)"), R, U32, "w_w")
+        l3 = load_list("l3", offs3)
+        xt_sc = load_scale_rows("xt_sc", xt_scales)
+        w_sc = load_scale_rows("w_sc", w_scales)
+        l5 = load_list("l5", offs5)
+        l6 = load_list("l6", offs6)
+        sa_sb = sb.tile([P, PACK], F32, name="sa_sb")
+        nc.sync.dma_start(sa_sb[:], sa.rearrange("(p t) o -> p (t o)", t=PACK))
+        vs_w = load_words(nc.sync, "vs_w", vs_words[0], S, U16, "vs_w")
+        vs_sc = load_scale_rows("vs_sc", vs_scales)
+
+        xt_gw = sb.tile([P, J], U16, name="xt_gw", tag="picked_words2", align_bytes=64)
+        xt_gs = sb.tile([P, J], U8, name="xt_gs", tag="picked_scales2", align_bytes=64)
+        nc.vector.tensor_copy(xt_gw[:], xt_w[:].indirect(l1[:]))
+        nc.vector.tensor_copy(xt_gs[:], xt_sc[:].indirect(l1[:]))
+        w_w_d = deal(nc.vector.tensor_copy, "w_w_d", w_w, U32, "dealt_words")
+        w_sc_d = deal(nc.vector.tensor_copy, "w_sc_d", w_sc, U8, "dealt_scales")
+
+        a_sb = []
+        for t in range(PACK):
+            a_ps = psum.tile([P, J], F32, name="a_ps%d" % t, tag="bank%d" % (PACK + t))
+            nc.tensor.matmul_mx(
+                out=a_ps[:], lhsT=w_w_d[:, t, :].bitcast(FP8X4), lhsT_scale=w_sc_d[:, t, :],
+                rhs=xt_gw[:].bitcast(FP4X4), rhs_scale=xt_gs[:], start=True, stop=True,
+            )
+            a_t = sb.tile([P, J], F32, name="a_sb%d" % t, tag="a_sb%d" % t, align_bytes=64)
+            nc.vector.tensor_copy(a_t[:], a_ps[:])
+            a_sb.append(a_t)
+
+        pw = [sb.tile([P, C], F32, name="pw%d" % i, tag="wide%d" % i, align_bytes=64) for i in range(2)]
+        for board in pw:
+            nc.vector.memset(board[:], 0.0)
+
+        vs_gw = sb.tile([P, N], U16, name="vs_gw", tag="picked_words2", align_bytes=64)
+        vs_gs = sb.tile([P, N], U8, name="vs_gs", tag="picked_scales2", align_bytes=64)
+        nc.vector.tensor_copy(vs_gw[:], vs_w[:].indirect(l6[:]))
+        nc.vector.tensor_copy(vs_gs[:], vs_sc[:].indirect(l6[:]))
+
+        pg = [sb.tile([P, C], F32, name="pg%d" % t) for t in range(PACK)]
+        for t in range(PACK):
+            board = pw[t % 2]
+            nc.scalar.activation(board[:].indirect(l3[:]), a_sb[t][:], COPY)
+            nc.vector.tensor_tensor(pg[t][:, 1:C], board[:, 1:C], pv[t][:, 0 : C - 1], SUB)
+            nc.vector.tensor_copy(pg[t][:, 0:1], board[:, 0:1])
+
+        hid = sb.tile([P, 2, PACK, HALF], BF16, name="hid", tag="a_sb%d" % (PACK - 1), align_bytes=64)
+        for h in range(2):
+            for t in range(PACK):
+                nc.scalar.activation(hid[:, h, t, :], pg[t][:].indirect(entries(l5, h * HALF, HALF)), COPY, scale=sa_sb[:, t : t + 1])
+            woven = sb.tile([P, HALF, PACK], BF16, name="woven%d" % h, align_bytes=64)
+            nc.vector.tensor_copy(woven[:], hid[:, h, :, :].rearrange("p t o -> p o t"))
+            hq_w = sb.tile([P, HALF], U32, name="hq_w%d" % h, align_bytes=64)
+            hq_s = sb.tile([P, HALF], U8, name="hq_s%d" % h, align_bytes=64)
+            nc.vector.quantize_mx(out=hq_w[:].bitcast(FP8X4), scales=hq_s[:], in_=woven[:].rearrange("p o t -> p (o t)"))
+            for nb in range(N // P):
+                rows = slice(nb * P, (nb + 1) * P)
+                y_ps = psum.tile([P, HALF], F32, name="y_ps%d%d" % (h, nb), tag="bank%d" % (2 * h + nb))
+                nc.tensor.matmul_mx(
+                    out=y_ps[:], lhsT=vs_gw[:, rows].bitcast(FP4X4), lhsT_scale=vs_gs[:, rows],
+                    rhs=hq_w[:].bitcast(FP8X4), rhs_scale=hq_s[:], start=True, stop=True,
+                )
+                y_sb = sb.tile([P, HALF], F32, name="y_sb%d%d" % (h, nb))
+                if h == 1 and nb == 1:
+                    nc.scalar.copy(y_sb[:], y_ps[:])
+                    nc.scalar.dma_start(out[rows, h * HALF : (h + 1) * HALF], y_sb[:])
+                else:
+                    nc.vector.tensor_copy(y_sb[:], y_ps[:])
+                    nc.sync.dma_start(out[rows, h * HALF : (h + 1) * HALF], y_sb[:])

@@ -21,6 +21,9 @@ PACK = 4
 QUADS = 4
 NOTE_PIECES = (128, 128, 256)
 HALF = O // 2
+EARLY = 2
+QUARTER = O // 4
+EIGHTH = O // 8
 
 
 def tile_picked_tokens_plain_two_lagged_store_plain_kernel(
@@ -38,12 +41,12 @@ def tile_picked_tokens_plain_two_lagged_store_plain_kernel(
             nc.sync.dma_start(tl[:], src)
             return tl
 
-        def load_scale_rows(name, src):
+        def load_scale_rows(queues, name, src):
             width = src.shape[2]
-            plane = sb.tile([P, width], U8, name=name, align_bytes=64)
+            plane = sb.tile([P, width], U8, name=name, tag=name, align_bytes=64)
             for q in range(QUADS):
                 rows = src[0, 4 * q : 4 * q + 4, :].bitcast(I32)
-                nc.sync.dma_start(plane[32 * q : 32 * q + 32, :].bitcast(I32), rows.partition_broadcast(8))
+                queues[q].dma_start(plane[32 * q : 32 * q + 32, :].bitcast(I32), rows.partition_broadcast(8))
             return plane
 
         def load_words(queue, name, src, width, dtype, tag):
@@ -51,76 +54,87 @@ def tile_picked_tokens_plain_two_lagged_store_plain_kernel(
             queue.dma_start(tl[:].bitcast(I32), src.bitcast(I32))
             return tl
 
-        def deal(engine_copy, name, src, dtype, tag):
+        def deal(engine_copy, name, src, dtype, run, tag):
             dealt = sb.tile([P, PACK, P], dtype, name=name, tag=tag, align_bytes=64)
-            engine_copy(dealt[:].rearrange("p t m -> p m t"), src[:].rearrange("p (m t) -> p m t", t=PACK))
+            engine_copy(
+                dealt[:].rearrange("p t (c i) -> p c t i", i=run),
+                src[:].rearrange("p (c i t) -> p c t i", i=run, t=PACK),
+            )
             return dealt
 
         def entries(tl, first, count):
             return tl[:, first // 16 : (first + count) // 16]
 
         w2s_stage = sb.tile([P, QUADS, R // 4], I32, name="w2s_stage")
-        nc.sync.dma_start(w2s_stage[0:4, :, :], w2_scales[0].rearrange("(q j) n -> j q n", j=4).bitcast(I32))
+        nc.scalar.dma_start(w2s_stage[0:4, :, :], w2_scales[0].rearrange("(q j) n -> j q n", j=4).bitcast(I32))
         l2 = load_list("l2", offs2)
-        xo_sc = load_scale_rows("xo_sc", xo_scales)
         w2_w = load_words(nc.scalar, "w2_w", w2_words[0], R, U16, "w2_w")
-        xo_w = load_words(nc.scalar, "xo_w", xo_words[0].rearrange("p n t -> p (n t)"), M, U32, "wide0")
+        xo_sc = load_scale_rows((nc.sync, nc.sync, nc.scalar, nc.scalar), "xo_sc", xo_scales)
+        xo_w = load_words(nc.sync, "xo_w", xo_words[0].rearrange("p n t -> p (n t)"), M, U32, "wide0")
         l4 = load_list("l4", offs4)
 
         w2_sc = sb.tile([P, R], U8, name="w2_sc", align_bytes=64)
         nc.vector.memset(w2_sc[:].bitcast(I32), 0)
-        pv = [sb.tile([P, C], F32, name="pv%d" % t) for t in range(PACK - 1)]
+        pv = [sb.tile([P, C], F32, name="pv%d" % t) for t in range(EARLY)]
         for board in pv:
-            nc.vector.memset(board[:], 0.0)
+            nc.vector.memset(board[:].bitcast(I32), 0)
         for q in range(QUADS):
             nc.vector.tensor_copy(w2_sc[32 * q : 32 * q + 4, :].bitcast(I32), w2s_stage[0:4, q, :])
-        w2_sc_d = deal(nc.vector.tensor_copy, "w2_sc_d", w2_sc, U8, "dealt_scales")
-        w2_w_d = deal(nc.scalar.copy, "w2_w_d", w2_w, U16, "dealt_words")
+        w2_sc_d = deal(nc.vector.tensor_copy, "w2_sc_d", w2_sc, U8, 16, "dealt_scales")
+        w2_w_d = deal(nc.scalar.copy, "w2_w_d", w2_w, U16, 8, "dealt_words")
 
-        b_sb = [sb.tile([P, J], F32, name="b_sb%d" % t) for t in range(PACK)]
-        b_ps = [psum.tile([P, J], F32, name="b_ps%d" % t, tag="bank%d" % t) for t in range(PACK)]
+        b_sb = [sb.tile([P, J], F32, name="b_sb%d" % t, tag="b_sb%d" % t, align_bytes=64) for t in range(PACK)]
+        late_ps = [psum.tile([P, J], F32, name="late_ps%d" % t, tag="bank%d" % (2 + t)) for t in range(EARLY, PACK)]
         first = 0
         for piece, count in enumerate(NOTE_PIECES):
             cols = slice(first, first + count)
-            xo_gs = sb.tile([P, count], U8, name="xo_gs%d" % piece, tag="picked_scales%d" % piece, align_bytes=64)
-            xo_gw = sb.tile([P, count], U32, name="xo_gw%d" % piece, tag="picked_words%d" % piece, align_bytes=64)
+            xo_gs = sb.tile([P, count], U8, name="xo_gs%d" % piece, tag="picked_scales%d" % (piece % 2), align_bytes=64)
+            xo_gw = sb.tile([P, count], U32, name="xo_gw%d" % piece, tag="picked_words%d" % (piece % 2), align_bytes=64)
             nc.vector.tensor_copy(xo_gs[:], xo_sc[:].indirect(entries(l2, first, count)))
             nc.vector.tensor_copy(xo_gw[:], xo_w[:].indirect(entries(l2, first, count)))
             for t in range(PACK):
+                if t < EARLY:
+                    early_ps = psum.tile([P, count], F32, name="early_ps%d%d" % (piece, t), tag="bank%d" % (2 * (piece % 2) + t))
+                    b_ps = early_ps[:]
+                else:
+                    b_ps = late_ps[t - EARLY][:, cols]
                 nc.tensor.matmul_mx(
-                    out=b_ps[t][:, cols], lhsT=w2_w_d[:, t, :].bitcast(FP4X4), lhsT_scale=w2_sc_d[:, t, :],
+                    out=b_ps, lhsT=w2_w_d[:, t, :].bitcast(FP4X4), lhsT_scale=w2_sc_d[:, t, :],
                     rhs=xo_gw[:].bitcast(FP8X4), rhs_scale=xo_gs[:], start=True, stop=True,
                 )
-                nc.vector.tensor_copy(b_sb[t][:, cols], b_ps[t][:, cols])
-                if len(pv) == t:
-                    pv.append(sb.tile([P, C], F32, name="pv%d" % t, tag="picked_words0", align_bytes=64))
-                    nc.vector.memset(pv[t][:], 0.0)
-                nc.scalar.activation(pv[t][:].indirect(entries(l4, first, count)), b_sb[t][:, cols], COPY)
+                if t < EARLY:
+                    nc.vector.tensor_copy(b_sb[t][:, cols], b_ps)
+                    nc.scalar.activation(pv[t][:].indirect(entries(l4, first, count)), b_sb[t][:, cols], COPY)
             first = first + count
+        for t, tag in ((2, "xo_sc"), (3, "wide0")):
+            nc.vector.tensor_copy(b_sb[t][:], late_ps[t - EARLY][:])
+            pv.append(sb.tile([P, C], F32, name="pv%d" % t, tag=tag, align_bytes=64))
+            nc.vector.memset(pv[t][:].bitcast(I32), 0)
+            nc.scalar.activation(pv[t][:].indirect(l4[:]), b_sb[t][:], COPY)
 
         l1 = load_list("l1", offs)
         xt_w = load_words(nc.sync, "xt_w", xt_words[0], T, U16, "wide1")
         w_w = load_words(nc.sync, "w_w", w_words[0].rearrange("p n t -> p (n t)"), R, U32, "w_w")
         l3 = load_list("l3", offs3)
-        xt_sc = load_scale_rows("xt_sc", xt_scales)
-        w_sc = load_scale_rows("w_sc", w_scales)
+        xt_sc = load_scale_rows((nc.sync,) * QUADS, "xt_sc", xt_scales)
+        w_sc = load_scale_rows((nc.sync,) * QUADS, "w_sc", w_scales)
         l5 = load_list("l5", offs5)
         l6 = load_list("l6", offs6)
         sa_sb = sb.tile([P, PACK], F32, name="sa_sb")
         nc.sync.dma_start(sa_sb[:], sa.rearrange("(p t) o -> p (t o)", t=PACK))
         vs_w = load_words(nc.sync, "vs_w", vs_words[0], S, U16, "vs_w")
-        vs_sc = load_scale_rows("vs_sc", vs_scales)
+        vs_sc = load_scale_rows((nc.sync,) * QUADS, "vs_sc", vs_scales)
 
-        xt_gw = sb.tile([P, J], U16, name="xt_gw", tag="picked_words2", align_bytes=64)
-        xt_gs = sb.tile([P, J], U8, name="xt_gs", tag="picked_scales2", align_bytes=64)
+        xt_gw = sb.tile([P, J], U16, name="xt_gw", tag="picked_words0", align_bytes=64)
+        xt_gs = sb.tile([P, J], U8, name="xt_gs", tag="picked_scales0", align_bytes=64)
         nc.vector.tensor_copy(xt_gw[:], xt_w[:].indirect(l1[:]))
         nc.vector.tensor_copy(xt_gs[:], xt_sc[:].indirect(l1[:]))
-        w_w_d = deal(nc.vector.tensor_copy, "w_w_d", w_w, U32, "dealt_words")
-        w_sc_d = deal(nc.vector.tensor_copy, "w_sc_d", w_sc, U8, "dealt_scales")
+        w_w_d = deal(nc.vector.tensor_copy, "w_w_d", w_w, U32, 4, "dealt_words")
+        w_sc_d = deal(nc.vector.tensor_copy, "w_sc_d", w_sc, U8, 16, "dealt_scales")
 
         a_sb = []
         for t in range(PACK):
-            a_ps = psum.tile([P, J], F32, name="a_ps%d" % t, tag="bank%d" % (PACK + t))
+            a_ps = psum.tile([P, J], F32, name="a_ps%d" % t, tag="bank%d" % (6, 7, 2, 3)[t])
             nc.tensor.matmul_mx(
                 out=a_ps[:], lhsT=w_w_d[:, t, :].bitcast(FP8X4), lhsT_scale=w_sc_d[:, t, :],
                 rhs=xt_gw[:].bitcast(FP4X4), rhs_scale=xt_gs[:], start=True, stop=True,
@@ -129,12 +143,12 @@ def tile_picked_tokens_plain_two_lagged_store_plain_kernel(
             nc.vector.tensor_copy(a_t[:], a_ps[:])
             a_sb.append(a_t)
 
-        pw = [sb.tile([P, C], F32, name="pw%d" % i, tag="wide%d" % i, align_bytes=64) for i in range(2)]
+        pw = [sb.tile([P, C], F32, name="pw_" + tag, tag=tag, align_bytes=64) for tag in ("b_sb0", "wide1")]
         for board in pw:
-            nc.vector.memset(board[:], 0.0)
+            nc.vector.memset(board[:].bitcast(I32), 0)
 
-        vs_gw = sb.tile([P, N], U16, name="vs_gw", tag="picked_words2", align_bytes=64)
-        vs_gs = sb.tile([P, N], U8, name="vs_gs", tag="picked_scales2", align_bytes=64)
+        vs_gw = sb.tile([P, N], U16, name="vs_gw", tag="picked_words0", align_bytes=64)
+        vs_gs = sb.tile([P, N], U8, name="vs_gs", tag="picked_scales0", align_bytes=64)
         nc.vector.tensor_copy(vs_gw[:], vs_w[:].indirect(l6[:]))
         nc.vector.tensor_copy(vs_gs[:], vs_sc[:].indirect(l6[:]))
 
@@ -142,29 +156,45 @@ def tile_picked_tokens_plain_two_lagged_store_plain_kernel(
         for t in range(PACK):
             board = pw[t % 2]
             nc.scalar.activation(board[:].indirect(l3[:]), a_sb[t][:], COPY)
-            nc.vector.tensor_tensor(pg[t][:, 1:C], board[:, 1:C], pv[t][:, 0 : C - 1], SUB)
             nc.vector.tensor_copy(pg[t][:, 0:1], board[:, 0:1])
+            nc.vector.tensor_tensor(pg[t][:, 1:C], board[:, 1:C], pv[t][:, 0 : C - 1], SUB)
 
-        hid = sb.tile([P, 2, PACK, HALF], BF16, name="hid", tag="a_sb%d" % (PACK - 1), align_bytes=64)
-        for h in range(2):
-            for t in range(PACK):
-                nc.scalar.activation(hid[:, h, t, :], pg[t][:].indirect(entries(l5, h * HALF, HALF)), COPY, scale=sa_sb[:, t : t + 1])
-            woven = sb.tile([P, HALF, PACK], BF16, name="woven%d" % h, align_bytes=64)
-            nc.vector.tensor_copy(woven[:], hid[:, h, :, :].rearrange("p t o -> p o t"))
-            hq_w = sb.tile([P, HALF], U32, name="hq_w%d" % h, align_bytes=64)
-            hq_s = sb.tile([P, HALF], U8, name="hq_s%d" % h, align_bytes=64)
-            nc.vector.quantize_mx(out=hq_w[:].bitcast(FP8X4), scales=hq_s[:], in_=woven[:].rearrange("p o t -> p (o t)"))
+        hid = [sb.tile([P, PACK, HALF], BF16, name="hid_" + tag, tag=tag, align_bytes=64) for tag in ("a_sb3", "wide1")]
+        def weave(engine_copy, woven, h, first):
+            count = woven.shape[1]
+            engine_copy(
+                woven,
+                hid[h][:, :, first : first + count].rearrange("p t o -> p o t"),
+            )
+
+        def finish(engine_copy, queue, name, woven, first, count, bank):
+            hq_w = sb.tile([P, count], U32, name="hq_w" + name, align_bytes=64)
+            hq_s = sb.tile([P, count], U8, name="hq_s" + name, align_bytes=64)
+            nc.vector.quantize_mx(out=hq_w[:].bitcast(FP8X4), scales=hq_s[:], in_=woven.rearrange("p o t -> p (o t)"))
+            y_ps = psum.tile([P, N // P, count], F32, name="y_ps" + name, tag=bank)
             for nb in range(N // P):
                 rows = slice(nb * P, (nb + 1) * P)
-                y_ps = psum.tile([P, HALF], F32, name="y_ps%d%d" % (h, nb), tag="bank%d" % (2 * h + nb))
                 nc.tensor.matmul_mx(
-                    out=y_ps[:], lhsT=vs_gw[:, rows].bitcast(FP4X4), lhsT_scale=vs_gs[:, rows],
+                    out=y_ps[:, nb, :], lhsT=vs_gw[:, rows].bitcast(FP4X4), lhsT_scale=vs_gs[:, rows],
                     rhs=hq_w[:].bitcast(FP8X4), rhs_scale=hq_s[:], start=True, stop=True,
                 )
-                y_sb = sb.tile([P, HALF], F32, name="y_sb%d%d" % (h, nb))
-                if h == 1 and nb == 1:
-                    nc.scalar.copy(y_sb[:], y_ps[:])
-                    nc.scalar.dma_start(out[rows, h * HALF : (h + 1) * HALF], y_sb[:])
-                else:
-                    nc.vector.tensor_copy(y_sb[:], y_ps[:])
-                    nc.sync.dma_start(out[rows, h * HALF : (h + 1) * HALF], y_sb[:])
+            y_sb = sb.tile([P, N // P, count], F32, name="y_sb" + name)
+            engine_copy(y_sb[:], y_ps[:])
+            queue.dma_start(out[:, first : first + count].rearrange("(b p) o -> p b o", p=P), y_sb[:])
+
+        def fetch(h):
+            for t in range(PACK):
+                nc.scalar.activation(hid[h][:, t, :], pg[t][:].indirect(entries(l5, h * HALF, HALF)), COPY, scale=sa_sb[:, t : t + 1])
+
+        fetch(0)
+        woven_a = sb.tile([P, HALF, PACK], BF16, name="woven_a", tag="woven", align_bytes=64)
+        weave(nc.vector.tensor_copy, woven_a[:], 0, 0)
+        finish(nc.scalar.copy, nc.sync, "a", woven_a[:], 0, HALF, "bank0")
+        fetch(1)
+        woven_b = sb.tile([P, HALF, PACK], BF16, name="woven_b", tag="woven", align_bytes=64)
+        split = QUARTER + EIGHTH
+        weave(nc.vector.tensor_copy, woven_b[:, :QUARTER, :], 1, 0)
+        weave(nc.vector.tensor_copy, woven_b[:, QUARTER:split, :], 1, QUARTER)
+        weave(nc.scalar.copy, woven_b[:, split:, :], 1, split)
+        finish(nc.vector.tensor_copy, nc.sync, "b", woven_b[:, :QUARTER, :], HALF, QUARTER, "bank1")
+        finish(nc.scalar.copy, nc.scalar, "c", woven_b[:, QUARTER:, :], HALF + QUARTER, QUARTER, "bank4")

@@ -41,12 +41,12 @@ def tile_picked_tokens_plain_two_lagged_store_plain_kernel(
             nc.sync.dma_start(tl[:], src)
             return tl
 
-        def load_scale_rows(queues, name, src):
+        def load_scale_rows(name, src):
             width = src.shape[2]
             plane = sb.tile([P, width], U8, name=name, tag=name, align_bytes=64)
             for q in range(QUADS):
                 rows = src[0, 4 * q : 4 * q + 4, :].bitcast(I32)
-                queues[q].dma_start(plane[32 * q : 32 * q + 32, :].bitcast(I32), rows.partition_broadcast(8))
+                nc.sync.dma_start(plane[32 * q : 32 * q + 32, :].bitcast(I32), rows.partition_broadcast(8))
             return plane
 
         def load_words(queue, name, src, width, dtype, tag):
@@ -66,11 +66,11 @@ def tile_picked_tokens_plain_two_lagged_store_plain_kernel(
             return tl[:, first // 16 : (first + count) // 16]
 
         w2s_stage = sb.tile([P, QUADS, R // 4], I32, name="w2s_stage")
-        nc.scalar.dma_start(w2s_stage[0:4, :, :], w2_scales[0].rearrange("(q j) n -> j q n", j=4).bitcast(I32))
+        nc.sync.dma_start(w2s_stage[0:4, :, :], w2_scales[0].rearrange("(q j) n -> j q n", j=4).bitcast(I32))
         l2 = load_list("l2", offs2)
         w2_w = load_words(nc.scalar, "w2_w", w2_words[0], R, U16, "w2_w")
-        xo_sc = load_scale_rows((nc.sync, nc.sync, nc.scalar, nc.scalar), "xo_sc", xo_scales)
-        xo_w = load_words(nc.sync, "xo_w", xo_words[0].rearrange("p n t -> p (n t)"), M, U32, "wide0")
+        xo_sc = load_scale_rows("xo_sc", xo_scales)
+        xo_w = load_words(nc.scalar, "xo_w", xo_words[0].rearrange("p n t -> p (n t)"), M, U32, "wide0")
         l4 = load_list("l4", offs4)
 
         w2_sc = sb.tile([P, R], U8, name="w2_sc", align_bytes=64)
@@ -116,14 +116,14 @@ def tile_picked_tokens_plain_two_lagged_store_plain_kernel(
         xt_w = load_words(nc.sync, "xt_w", xt_words[0], T, U16, "wide1")
         w_w = load_words(nc.sync, "w_w", w_words[0].rearrange("p n t -> p (n t)"), R, U32, "w_w")
         l3 = load_list("l3", offs3)
-        xt_sc = load_scale_rows((nc.sync,) * QUADS, "xt_sc", xt_scales)
-        w_sc = load_scale_rows((nc.sync,) * QUADS, "w_sc", w_scales)
+        xt_sc = load_scale_rows("xt_sc", xt_scales)
+        w_sc = load_scale_rows("w_sc", w_scales)
         l5 = load_list("l5", offs5)
         l6 = load_list("l6", offs6)
         sa_sb = sb.tile([P, PACK], F32, name="sa_sb")
         nc.sync.dma_start(sa_sb[:], sa.rearrange("(p t) o -> p (t o)", t=PACK))
         vs_w = load_words(nc.sync, "vs_w", vs_words[0], S, U16, "vs_w")
-        vs_sc = load_scale_rows((nc.sync,) * QUADS, "vs_sc", vs_scales)
+        vs_sc = load_scale_rows("vs_sc", vs_scales)
 
         xt_gw = sb.tile([P, J], U16, name="xt_gw", tag="picked_words0", align_bytes=64)
         xt_gs = sb.tile([P, J], U8, name="xt_gs", tag="picked_scales0", align_bytes=64)

from contextlib import ExitStack

import concourse.mybir as mybir

K, J, R, T, Z, M, C, O, N, S = 512, 512, 512, 2048, 512, 1024, 1024, 512, 256, 1024
FLOPS = 2 * K * R * J + 2 * Z * R * J + 2 * R * N * O

F32 = mybir.dt.float32
BF16 = mybir.dt.bfloat16
I32 = mybir.dt.int32
U32 = mybir.dt.uint32
U16 = mybir.dt.uint16
U8 = mybir.dt.uint8
FP8X4 = mybir.dt.float8_e4m3fn_x4
FP4X4 = mybir.dt.float4_e2m1fn_x4
COPY = mybir.ActivationFunctionType.Copy
SUB = mybir.AluOpType.subtract

P = 128
PACK = 4
QUADS = 4
NOTE_PIECES = (128, 128, 256)
HALF = O // 2
EARLY = 2
QUARTER = O // 4
EIGHTH = O // 8


def tile_picked_tokens_plain_two_lagged_store_plain_kernel(
    tc, xt_words, xt_scales, w_words, w_scales, xo_words, xo_scales, w2_words, w2_scales,
    sa, vs_words, vs_scales, offs, offs2, offs3, offs4, offs5, offs6, out,
):
    nc = tc.nc
    with ExitStack() as ctx:
        lists = ctx.enter_context(tc.tile_pool(name="lists", bufs=1))
        sb = ctx.enter_context(tc.tile_pool(name="sb", bufs=1))
        psum = ctx.enter_context(tc.psum_pool(name="psum", bufs=1))

        def load_list(name, src):
            tl = lists.tile(list(src.shape), U16, name=name)
            nc.sync.dma_start(tl[:], src)
            return tl

        def load_scale_rows(name, src):
            width = src.shape[2]
            plane = sb.tile([P, width], U8, name=name, tag=name, align_bytes=64)
            for q in range(QUADS):
                rows = src[0, 4 * q : 4 * q + 4, :].bitcast(I32)
                nc.sync.dma_start(plane[32 * q : 32 * q + 32, :].bitcast(I32), rows.partition_broadcast(8))
            return plane

        def load_words(queue, name, src, width, dtype, tag):
            tl = sb.tile([P, width], dtype, name=name, tag=tag, align_bytes=64)
            queue.dma_start(tl[:].bitcast(I32), src.bitcast(I32))
            return tl

        def deal(engine_copy, name, src, dtype, run, tag):
            dealt = sb.tile([P, PACK, P], dtype, name=name, tag=tag, align_bytes=64)
            engine_copy(
                dealt[:].rearrange("p t (c i) -> p c t i", i=run),
                src[:].rearrange("p (c i t) -> p c t i", i=run, t=PACK),
            )
            return dealt

        def entries(tl, first, count):
            return tl[:, first // 16 : (first + count) // 16]

        w2s_stage = sb.tile([P, QUADS, R // 4], I32, name="w2s_stage")
        nc.sync.dma_start(w2s_stage[0:4, :, :], w2_scales[0].rearrange("(q j) n -> j q n", j=4).bitcast(I32))
        l2 = load_list("l2", offs2)
        w2_w = load_words(nc.scalar, "w2_w", w2_words[0], R, U16, "w2_w")
        xo_sc = load_scale_rows("xo_sc", xo_scales)
        xo_w = load_words(nc.scalar, "xo_w", xo_words[0].rearrange("p n t -> p (n t)"), M, U32, "wide0")
        l4 = load_list("l4", offs4)

        w2_sc = sb.tile([P, R], U8, name="w2_sc", align_bytes=64)
        nc.vector.memset(w2_sc[:].bitcast(I32), 0)
        pv = [sb.tile([P, C], F32, name="pv%d" % t) for t in range(EARLY)]
        for board in pv:
            nc.vector.memset(board[:].bitcast(I32), 0)
        for q in range(QUADS):
            nc.vector.tensor_copy(w2_sc[32 * q : 32 * q + 4, :].bitcast(I32), w2s_stage[0:4, q, :])
        w2_sc_d = deal(nc.vector.tensor_copy, "w2_sc_d", w2_sc, U8, 16, "dealt_scales")
        w2_w_d = deal(nc.scalar.copy, "w2_w_d", w2_w, U16, 8, "dealt_words")

        b_sb = [sb.tile([P, J], F32, name="b_sb%d" % t, tag="b_sb%d" % t, align_bytes=64) for t in range(PACK)]
        late_ps = [psum.tile([P, J], F32, name="late_ps%d" % t, tag="bank%d" % (2 + t)) for t in range(EARLY, PACK)]
        first = 0
        for piece, count in enumerate(NOTE_PIECES):
            cols = slice(first, first + count)
            xo_gs = sb.tile([P, count], U8, name="xo_gs%d" % piece, tag="picked_scales%d" % (piece % 2), align_bytes=64)
            xo_gw = sb.tile([P, count], U32, name="xo_gw%d" % piece, tag="picked_words%d" % (piece % 2), align_bytes=64)
            nc.vector.tensor_copy(xo_gs[:], xo_sc[:].indirect(entries(l2, first, count)))
            nc.vector.tensor_copy(xo_gw[:], xo_w[:].indirect(entries(l2, first, count)))
            for t in range(PACK):
                if t < EARLY:
                    early_ps = psum.tile([P, count], F32, name="early_ps%d%d" % (piece, t), tag="bank%d" % (2 * (piece % 2) + t))
                    b_ps = early_ps[:]
                else:
                    b_ps = late_ps[t - EARLY][:, cols]
                nc.tensor.matmul_mx(
                    out=b_ps, lhsT=w2_w_d[:, t, :].bitcast(FP4X4), lhsT_scale=w2_sc_d[:, t, :],
                    rhs=xo_gw[:].bitcast(FP8X4), rhs_scale=xo_gs[:], start=True, stop=True,
                )
                if t < EARLY:
                    nc.vector.tensor_copy(b_sb[t][:, cols], b_ps)
                    nc.scalar.activation(pv[t][:].indirect(entries(l4, first, count)), b_sb[t][:, cols], COPY)
            first = first + count
        for t, tag in ((2, "xo_sc"), (3, "wide0")):
            nc.vector.tensor_copy(b_sb[t][:], late_ps[t - EARLY][:])
            pv.append(sb.tile([P, C], F32, name="pv%d" % t, tag=tag, align_bytes=64))
            nc.vector.memset(pv[t][:].bitcast(I32), 0)
            nc.scalar.activation(pv[t][:].indirect(l4[:]), b_sb[t][:], COPY)

        l1 = load_list("l1", offs)
        xt_w = load_words(nc.sync, "xt_w", xt_words[0], T, U16, "wide1")
        w_w = load_words(nc.sync, "w_w", w_words[0].rearrange("p n t -> p (n t)"), R, U32, "w_w")
        l3 = load_list("l3", offs3)
        xt_sc = load_scale_rows("xt_sc", xt_scales)
        w_sc = load_scale_rows("w_sc", w_scales)
        l5 = load_list("l5", offs5)
        l6 = load_list("l6", offs6)
        sa_sb = sb.tile([P, PACK], F32, name="sa_sb")
        nc.sync.dma_start(sa_sb[:], sa.rearrange("(p t) o -> p (t o)", t=PACK))
        vs_w = load_words(nc.sync, "vs_w", vs_words[0], S, U16, "vs_w")
        vs_sc = load_scale_rows("vs_sc", vs_scales)

        xt_gw = sb.tile([P, J], U16, name="xt_gw", tag="picked_words0", align_bytes=64)
        xt_gs = sb.tile([P, J], U8, name="xt_gs", tag="picked_scales0", align_bytes=64)
        nc.vector.tensor_copy(xt_gw[:], xt_w[:].indirect(l1[:]))
        nc.vector.tensor_copy(xt_gs[:], xt_sc[:].indirect(l1[:]))
        w_w_d = deal(nc.vector.tensor_copy, "w_w_d", w_w, U32, 4, "dealt_words")
        w_sc_d = deal(nc.vector.tensor_copy, "w_sc_d", w_sc, U8, 16, "dealt_scales")

        a_sb = []
        for t in range(PACK):
            a_ps = psum.tile([P, J], F32, name="a_ps%d" % t, tag="bank%d" % (6, 7, 2, 3)[t])
            nc.tensor.matmul_mx(
                out=a_ps[:], lhsT=w_w_d[:, t, :].bitcast(FP8X4), lhsT_scale=w_sc_d[:, t, :],
                rhs=xt_gw[:].bitcast(FP4X4), rhs_scale=xt_gs[:], start=True, stop=True,
            )
            a_t = sb.tile([P, J], F32, name="a_sb%d" % t, tag="a_sb%d" % t, align_bytes=64)
            nc.vector.tensor_copy(a_t[:], a_ps[:])
            a_sb.append(a_t)

        pw = [sb.tile([P, C], F32, name="pw_" + tag, tag=tag, align_bytes=64) for tag in ("b_sb0", "wide1")]
        for board in pw:
            nc.vector.memset(board[:].bitcast(I32), 0)

        vs_gw = sb.tile([P, N], U16, name="vs_gw", tag="picked_words0", align_bytes=64)
        vs_gs = sb.tile([P, N], U8, name="vs_gs", tag="picked_scales0", align_bytes=64)
        nc.vector.tensor_copy(vs_gw[:], vs_w[:].indirect(l6[:]))
        nc.vector.tensor_copy(vs_gs[:], vs_sc[:].indirect(l6[:]))

        pg = [sb.tile([P, C], F32, name="pg%d" % t) for t in range(PACK)]
        for t in range(PACK):
            board = pw[t % 2]
            nc.scalar.activation(board[:].indirect(l3[:]), a_sb[t][:], COPY)
            nc.vector.tensor_copy(pg[t][:, 0:1], board[:, 0:1])
            nc.vector.tensor_tensor(pg[t][:, 1:C], board[:, 1:C], pv[t][:, 0 : C - 1], SUB)

        hid = [sb.tile([P, PACK, HALF], BF16, name="hid_" + tag, tag=tag, align_bytes=64) for tag in ("a_sb3", "wide1")]
        def weave(engine_copy, woven, h, first):
            count = woven.shape[1]
            engine_copy(
                woven,
                hid[h][:, :, first : first + count].rearrange("p t o -> p o t"),
            )

        def finish(engine_copy, queue, name, woven, first, count, bank):
            hq_w = sb.tile([P, count], U32, name="hq_w" + name, align_bytes=64)
            hq_s = sb.tile([P, count], U8, name="hq_s" + name, align_bytes=64)
            nc.vector.quantize_mx(out=hq_w[:].bitcast(FP8X4), scales=hq_s[:], in_=woven.rearrange("p o t -> p (o t)"))
            y_ps = psum.tile([P, N // P, count], F32, name="y_ps" + name, tag=bank)
            for nb in range(N // P):
                rows = slice(nb * P, (nb + 1) * P)
                nc.tensor.matmul_mx(
                    out=y_ps[:, nb, :], lhsT=vs_gw[:, rows].bitcast(FP4X4), lhsT_scale=vs_gs[:, rows],
                    rhs=hq_w[:].bitcast(FP8X4), rhs_scale=hq_s[:], start=True, stop=True,
                )
            y_sb = sb.tile([P, N // P, count], F32, name="y_sb" + name)
            engine_copy(y_sb[:], y_ps[:])
            queue.dma_start(out[:, first : first + count].rearrange("(b p) o -> p b o", p=P), y_sb[:])

        def fetch(h):
            for t in range(PACK):
                nc.scalar.activation(hid[h][:, t, :], pg[t][:].indirect(entries(l5, h * HALF, HALF)), COPY, scale=sa_sb[:, t : t + 1])

        fetch(0)
        woven_a = sb.tile([P, HALF, PACK], BF16, name="woven_a", tag="woven", align_bytes=64)
        weave(nc.vector.tensor_copy, woven_a[:], 0, 0)
        finish(nc.scalar.copy, nc.sync, "a", woven_a[:], 0, HALF, "bank0")
        fetch(1)
        woven_b = sb.tile([P, HALF, PACK], BF16, name="woven_b", tag="woven", align_bytes=64)
        split = QUARTER + EIGHTH
        weave(nc.vector.tensor_copy, woven_b[:, :QUARTER, :], 1, 0)
        weave(nc.vector.tensor_copy, woven_b[:, QUARTER:split, :], 1, QUARTER)
        weave(nc.scalar.copy, woven_b[:, split:, :], 1, split)
        finish(nc.vector.tensor_copy, nc.sync, "b", woven_b[:, :QUARTER, :], HALF, QUARTER, "bank1")
        finish(nc.scalar.copy, nc.scalar, "c", woven_b[:, QUARTER:, :], HALF + QUARTER, QUARTER, "bank4")
